import numpy as np
import ml_dtypes


def mxq(x, axis, fmt="e4m3"):
    dtype, down = {"e4m3": (ml_dtypes.float8_e4m3fn, 7), "e5m2": (ml_dtypes.float8_e5m2, 14)}[fmt]
    v = np.moveaxis(np.asarray(x, np.float32).astype(ml_dtypes.bfloat16).astype(np.float64), axis, -1)
    blocks = v.reshape(v.shape[:-1] + (-1, 32))
    amax = np.abs(blocks).max(-1, keepdims=True)
    byte = np.maximum(np.where(amax > 0, np.frexp(amax)[1] - 1 + 127, 0) - down, 1)
    scale = np.exp2(byte - 127.0)
    codes = (blocks / scale).astype(np.float32).astype(dtype).astype(np.float64)
    return np.moveaxis((codes * scale).reshape(v.shape), -1, axis)


WIDE = False


def mx_kscale(k, group=512):
    if not WIDE:
        return np.ones(k)
    levels = np.array([10, -10, 5, -5, 0])
    if group != 512:
        return np.exp2(np.random.permutation(np.resize(levels, k // group))).repeat(group)
    if k % 512:
        return np.exp2(np.random.permutation(np.resize(levels, k // 32))).repeat(32)
    a = np.empty((k // 512, 16))
    for p in range(k // 512):
        a[p, :8] = np.random.permutation(np.resize(levels, 8))
        for g in range(8):
            far = levels[np.abs(levels - a[p, g]) >= 10]
            a[p, g + 8] = far[np.random.randint(len(far))]
    return np.exp2(a.ravel()).repeat(32)


def f64(x):
    return np.asarray(x).astype(np.float64)


E2M1 = np.array([0.0, 0.5, 1.0, 1.5, 2.0, 3.0, 4.0, 6.0, -0.0, -0.5, -1.0, -1.5, -2.0, -3.0, -4.0, -6.0])


def pack_group(w):
    k, n = w.shape
    w = f64(np.asarray(w, np.float32).astype(ml_dtypes.bfloat16)).reshape(k // 32, 32, n)
    amax = np.abs(w).max(1)
    mant, ex = np.frexp(amax / 6.0)
    byte = np.clip(np.where(amax > 0, np.where(mant > 0.5, ex, ex - 1) + 127, 1), 1, 254)
    scaled = (w * np.exp2(127.0 - byte)[:, None, :]).reshape(k, n).astype(np.float32)
    c = np.ascontiguousarray(scaled.reshape(k // 4, 4, n).transpose(0, 2, 1)).astype(ml_dtypes.float4_e2m1fn).view(np.uint8) & 0xF
    return np.ascontiguousarray((c[..., 0::2] | (c[..., 1::2] << 4)).reshape(k // 4, 2 * n)), byte.astype(np.uint8)


def unpack_group(words, scales):
    p, n = words.shape[0], scales.shape[1]
    words = np.ascontiguousarray(words).reshape(p, n, 2)
    nib = np.empty((p, n, 4), np.uint8)
    nib[..., 0::2] = words & 0xF
    nib[..., 1::2] = words >> 4
    return E2M1[nib].transpose(0, 2, 1).reshape(4 * p, n) * np.repeat(np.exp2(scales.astype(np.float64) - 127.0), 32, axis=0)


G, D, M, N = 4, 256, 256, 512


def setup_inputs():
    n = np.random.standard_normal
    s = mx_kscale(D, 0)[:, None]
    w_ = [pack_group(w) for w in n((G, D, M)) / np.sqrt(D) / s]
    return {
        "x": (n((G, D, N)) * s).astype(np.float32),
        "w_words": np.stack([w[0] for w in w_]),
        "w_scales": np.stack([w[1] for w in w_]),
    }


def reference(x, w_words, w_scales):
    xq = mxq(f64(x), 1, "e4m3")
    y = np.stack([unpack_group(w_words[g], w_scales[g]) for g in range(G)]).transpose(0, 2, 1) @ xq
    y = 1.0 / (1.0 + np.exp(-(y)))
    return y

@@ -1,0 +1,103 @@
+from contextlib import ExitStack
+
+import concourse.mybir as mybir
+
+G, D, M, N = 4, 256, 256, 512
+FLOPS = 2 * G * D * M * N
+
+F32 = mybir.dt.float32
+BF16 = mybir.dt.bfloat16
+I32 = mybir.dt.int32
+U32 = mybir.dt.uint32
+U8 = mybir.dt.uint8
+FP8X4 = mybir.dt.float8_e4m3fn_x4
+FP4X4 = mybir.dt.float4_e2m1fn_x4
+SIGMOID = mybir.ActivationFunctionType.Sigmoid
+
+P = 128
+PACK = 4
+ROWS = D // PACK
+SIDE = P // ROWS
+PAIRS = G // SIDE
+M_TILE = 128
+M_TILES = M // M_TILE
+CHUNK = 256
+CHUNKS = N // CHUNK
+PIECE = 128
+
+
+def tile_rows_glin_sigmoid_kernel(tc, x, w_words, w_scales, out):
+    nc = tc.nc
+    x_v = x.rearrange("(s c) (p j) n -> s (c p) j n", c=SIDE, j=PACK)
+    words_v = w_words.rearrange("(s c) p b -> (c p) s b", c=SIDE)
+    scales_v = w_scales.rearrange("(s c) (h r) m -> (c h) r s m", c=SIDE, r=4)
+
+    with ExitStack() as ctx:
+        sb = ctx.enter_context(tc.tile_pool(name="sb", bufs=1))
+        ps = ctx.enter_context(tc.psum_pool(name="ps", bufs=1))
+        ctx.enter_context(tc.manual_schedule())
+
+        words = sb.tile([P, PAIRS, 2 * M], U8, align_bytes=64, name="words")
+        wsc = sb.tile([P, PAIRS, M], U8, align_bytes=64, name="wsc")
+        warm = sb.tile([P, 8], F32, name="warm")
+        warm_out = sb.tile([P, 8], F32, name="warm_out")
+        raw = {}
+        grouped = {}
+        codes = {}
+        xsc = {}
+        for s in range(PAIRS):
+            codes[s] = sb.tile([P, N], U32, align_bytes=64, name="codes%d" % s)
+            xsc[s] = sb.tile([P, N], U8, align_bytes=64, name="xsc%d" % s)
+            grouped[s] = sb.tile([P, N, PACK], BF16, align_bytes=64, name="grouped%d" % s)
+            for h in range(CHUNKS):
+                raw[s, h] = sb.tile([P, PACK, CHUNK], F32, align_bytes=64, name="raw%d_%d" % (s, h))
+
+        nc.vector.memset(wsc[:].rearrange("p s m -> p (s m)").bitcast(I32), 0)
+        nc.vector.memset(warm[:], 0.0)
+
+        for s in range(PAIRS):
+            for h in range(CHUNKS):
+                nc.sync.dma_start(out=raw[s, h][:], in_=x_v[s, :, :, h * CHUNK:(h + 1) * CHUNK])
+
+        nc.scalar.dma_start(out=words[:].bitcast(I32), in_=words_v.bitcast(I32))
+        for q in range(4):
+            nc.scalar.dma_start(out=wsc[32 * q:32 * q + 4, :, :].bitcast(I32), in_=scales_v[q].bitcast(I32))
+        nc.scalar.activation(out=warm_out[:], in_=warm[:], func=SIGMOID)
+
+        def interleave(s, c0):
+            h, o = divmod(c0, CHUNK)
+            nc.vector.tensor_copy(
+                out=grouped[s][:, c0:c0 + PIECE, :].rearrange("p (c i) t -> p c t i", i=4),
+                in_=raw[s, h][:, :, o:o + PIECE].rearrange("p t (c i) -> p c t i", i=4),
+            )
+
+        def quantise(s, c0):
+            nc.vector.quantize_mx(
+                out=codes[s][:, c0:c0 + PIECE].bitcast(FP8X4),
+                scales=xsc[s][:, c0:c0 + PIECE],
+                in_=grouped[s][:, c0:c0 + PIECE, :].rearrange("p n t -> p (n t)"),
+            )
+
+        for s in range(PAIRS):
+            for h in range(CHUNKS):
+                cols = range(h * CHUNK, (h + 1) * CHUNK, PIECE)
+                for c0 in cols:
+                    interleave(s, c0)
+                for c0 in cols:
+                    quantise(s, c0)
+            for mt in range(M_TILES):
+                for c in range(SIDE):
+                    rows = slice(c * ROWS, (c + 1) * ROWS)
+                    acc = ps.tile([M_TILE, N], F32, name="acc%d_%d_%d" % (s, mt, c))
+                    nc.tensor.matmul_mx(
+                        out=acc[:],
+                        lhsT=words[rows, s, 2 * M_TILE * mt:2 * M_TILE * (mt + 1)].bitcast(FP4X4),
+                        lhsT_scale=wsc[rows, s, M_TILE * mt:M_TILE * (mt + 1)],
+                        rhs=codes[s][rows, :].bitcast(FP8X4),
+                        rhs_scale=xsc[s][rows, :],
+                        start=True,
+                        stop=True,
+                    )
+                    res = sb.tile([M_TILE, N], F32, name="res%d_%d_%d" % (s, mt, c))
+                    nc.scalar.activation(out=res[:], in_=acc[:], func=SIGMOID)
+                    nc.sync.dma_start(out=out[SIDE * s + c, M_TILE * mt:M_TILE * (mt + 1), :], in_=res[:])

@@ -22,8 +22,11 @@ PAIRS = G // SIDE
 M_TILE = 128
 M_TILES = M // M_TILE
 CHUNK = 256
-CHUNKS = N // CHUNK
+HALVES = N // CHUNK
+CHUNKS = PAIRS * HALVES
 PIECE = 128
+WINDOW = 512
+LEAD = WINDOW - CHUNK
 
 
 def tile_rows_glin_sigmoid_kernel(tc, x, w_words, w_scales, out):
@@ -31,6 +34,7 @@ def tile_rows_glin_sigmoid_kernel(tc, x, w_words, w_scales, out):
     x_v = x.rearrange("(s c) (p j) n -> s (c p) j n", c=SIDE, j=PACK)
     words_v = w_words.rearrange("(s c) p b -> (c p) s b", c=SIDE)
     scales_v = w_scales.rearrange("(s c) (h r) m -> (c h) r s m", c=SIDE, r=4)
+    out_v = out.rearrange("(s c) (t p) n -> s p c t n", c=SIDE, p=M_TILE)
 
     with ExitStack() as ctx:
         sb = ctx.enter_context(tc.tile_pool(name="sb", bufs=1))
@@ -41,63 +45,76 @@ def tile_rows_glin_sigmoid_kernel(tc, x, w_words, w_scales, out):
         wsc = sb.tile([P, PAIRS, M], U8, align_bytes=64, name="wsc")
         warm = sb.tile([P, 8], F32, name="warm")
         warm_out = sb.tile([P, 8], F32, name="warm_out")
-        raw = {}
-        grouped = {}
-        codes = {}
-        xsc = {}
-        for s in range(PAIRS):
-            codes[s] = sb.tile([P, N], U32, align_bytes=64, name="codes%d" % s)
-            xsc[s] = sb.tile([P, N], U8, align_bytes=64, name="xsc%d" % s)
-            grouped[s] = sb.tile([P, N, PACK], BF16, align_bytes=64, name="grouped%d" % s)
-            for h in range(CHUNKS):
-                raw[s, h] = sb.tile([P, PACK, CHUNK], F32, align_bytes=64, name="raw%d_%d" % (s, h))
+        codes = sb.tile([P, LEAD + CHUNKS * CHUNK], U32, align_bytes=64, name="codes")
+        xsc = sb.tile([P, LEAD + CHUNKS * CHUNK], U8, align_bytes=64, name="xsc")
+        raw = []
+        grouped = []
+        res = []
+        for k in range(CHUNKS):
+            raw.append(sb.tile([P, PACK, CHUNK], F32, align_bytes=64, name="raw%d" % k))
+            grouped.append(sb.tile([P, CHUNK, PACK], BF16, align_bytes=64, name="grouped%d" % k))
+            res.append(sb.tile([P, SIDE, M_TILES, CHUNK], F32, align_bytes=64, name="res%d" % k))
+        acc = {}
+        for b in range(2):
+            for mt in range(M_TILES):
+                for c in range(SIDE):
+                    acc[b, mt, c] = ps.tile([M_TILE, WINDOW], F32, name="acc%d_%d_%d" % (b, mt, c))
 
         nc.vector.memset(wsc[:].rearrange("p s m -> p (s m)").bitcast(I32), 0)
         nc.vector.memset(warm[:], 0.0)
-
-        for s in range(PAIRS):
-            for h in range(CHUNKS):
-                nc.sync.dma_start(out=raw[s, h][:], in_=x_v[s, :, :, h * CHUNK:(h + 1) * CHUNK])
-
-        nc.scalar.dma_start(out=words[:].bitcast(I32), in_=words_v.bitcast(I32))
-        for q in range(4):
-            nc.scalar.dma_start(out=wsc[32 * q:32 * q + 4, :, :].bitcast(I32), in_=scales_v[q].bitcast(I32))
+        nc.vector.memset(codes[:, 0:LEAD], 0)
+        nc.vector.memset(xsc[:, 0:LEAD].bitcast(I32), 0)
         nc.scalar.activation(out=warm_out[:], in_=warm[:], func=SIGMOID)
 
-        def interleave(s, c0):
-            h, o = divmod(c0, CHUNK)
+        def load(k):
+            s, h = divmod(k, HALVES)
+            nc.sync.dma_start(out=raw[k][:], in_=x_v[s, :, :, h * CHUNK:(h + 1) * CHUNK])
+
+        load(0)
+        nc.sync.dma_start(out=words[:].bitcast(I32), in_=words_v.bitcast(I32))
+        for q in range(4):
+            nc.sync.dma_start(out=wsc[32 * q:32 * q + 4, :, :].bitcast(I32), in_=scales_v[q].bitcast(I32))
+        for k in range(1, CHUNKS):
+            load(k)
+
+        def interleave(k, o):
             nc.vector.tensor_copy(
-                out=grouped[s][:, c0:c0 + PIECE, :].rearrange("p (c i) t -> p c t i", i=4),
-                in_=raw[s, h][:, :, o:o + PIECE].rearrange("p t (c i) -> p c t i", i=4),
+                out=grouped[k][:, o:o + PIECE, :].rearrange("p (c i) t -> p c t i", i=4),
+                in_=raw[k][:, :, o:o + PIECE].rearrange("p t (c i) -> p c t i", i=4),
             )
 
-        def quantise(s, c0):
+        def quantise(k, o):
+            c0 = LEAD + k * CHUNK + o
             nc.vector.quantize_mx(
-                out=codes[s][:, c0:c0 + PIECE].bitcast(FP8X4),
-                scales=xsc[s][:, c0:c0 + PIECE],
-                in_=grouped[s][:, c0:c0 + PIECE, :].rearrange("p n t -> p (n t)"),
+                out=codes[:, c0:c0 + PIECE].bitcast(FP8X4),
+                scales=xsc[:, c0:c0 + PIECE],
+                in_=grouped[k][:, o:o + PIECE, :].rearrange("p n t -> p (n t)"),
             )
 
-        for s in range(PAIRS):
-            for h in range(CHUNKS):
-                cols = range(h * CHUNK, (h + 1) * CHUNK, PIECE)
-                for c0 in cols:
-                    interleave(s, c0)
-                for c0 in cols:
-                    quantise(s, c0)
+        for k in range(CHUNKS):
+            s, h = divmod(k, HALVES)
+            cols = slice(h * CHUNK, (h + 1) * CHUNK)
+            window = slice(k * CHUNK, k * CHUNK + WINDOW)
+            for o in range(0, CHUNK, PIECE):
+                interleave(k, o)
+            for o in range(0, CHUNK, PIECE):
+                quantise(k, o)
+            split = k in (0, CHUNKS - 1)
             for mt in range(M_TILES):
                 for c in range(SIDE):
                     rows = slice(c * ROWS, (c + 1) * ROWS)
-                    acc = ps.tile([M_TILE, N], F32, name="acc%d_%d_%d" % (s, mt, c))
+                    bank = acc[k % 2, mt, c]
                     nc.tensor.matmul_mx(
-                        out=acc[:],
+                        out=bank[:],
                         lhsT=words[rows, s, 2 * M_TILE * mt:2 * M_TILE * (mt + 1)].bitcast(FP4X4),
                         lhsT_scale=wsc[rows, s, M_TILE * mt:M_TILE * (mt + 1)],
-                        rhs=codes[s][rows, :].bitcast(FP8X4),
-                        rhs_scale=xsc[s][rows, :],
+                        rhs=codes[rows, window].bitcast(FP8X4),
+                        rhs_scale=xsc[rows, window],
                         start=True,
                         stop=True,
                     )
-                    res = sb.tile([M_TILE, N], F32, name="res%d_%d_%d" % (s, mt, c))
-                    nc.scalar.activation(out=res[:], in_=acc[:], func=SIGMOID)
-                    nc.sync.dma_start(out=out[SIDE * s + c, M_TILE * mt:M_TILE * (mt + 1), :], in_=res[:])
+                    nc.scalar.activation(out=res[k][:, c, mt, :], in_=bank[:, LEAD:WINDOW], func=SIGMOID)
+                if split:
+                    nc.sync.dma_start(out=out_v[s, :, :, mt, cols], in_=res[k][:, :, mt, :])
+            if not split:
+                nc.sync.dma_start(out=out_v[s, :, :, :, cols], in_=res[k][:])

@@ -99,8 +99,8 @@ def tile_rows_glin_sigmoid_kernel(tc, x, w_words, w_scales, out):
                 interleave(k, o)
             for o in range(0, CHUNK, PIECE):
                 quantise(k, o)
-            split = k in (0, CHUNKS - 1)
             for mt in range(M_TILES):
+                last = k == CHUNKS - 1 and mt == M_TILES - 1
                 for c in range(SIDE):
                     rows = slice(c * ROWS, (c + 1) * ROWS)
                     bank = acc[k % 2, mt, c]
@@ -114,7 +114,7 @@ def tile_rows_glin_sigmoid_kernel(tc, x, w_words, w_scales, out):
                         stop=True,
                     )
                     nc.scalar.activation(out=res[k][:, c, mt, :], in_=bank[:, LEAD:WINDOW], func=SIGMOID)
-                if split:
+                    if last:
+                        nc.sync.dma_start(out=out_v[s, :, c, mt, cols], in_=res[k][:, c, mt, :])
+                if not last:
                     nc.sync.dma_start(out=out_v[s, :, :, mt, cols], in_=res[k][:, :, mt, :])
-            if not split:
-                nc.sync.dma_start(out=out_v[s, :, :, :, cols], in_=res[k][:])

@@ -43,8 +43,6 @@ def tile_rows_glin_sigmoid_kernel(tc, x, w_words, w_scales, out):
 
         words = sb.tile([P, PAIRS, 2 * M], U8, align_bytes=64, name="words")
         wsc = sb.tile([P, PAIRS, M], U8, align_bytes=64, name="wsc")
-        warm = sb.tile([P, 8], F32, name="warm")
-        warm_out = sb.tile([P, 8], F32, name="warm_out")
         codes = sb.tile([P, LEAD + CHUNKS * CHUNK], U32, align_bytes=64, name="codes")
         xsc = sb.tile([P, LEAD + CHUNKS * CHUNK], U8, align_bytes=64, name="xsc")
         raw = []
@@ -61,10 +59,8 @@ def tile_rows_glin_sigmoid_kernel(tc, x, w_words, w_scales, out):
                     acc[b, mt, c] = ps.tile([M_TILE, WINDOW], F32, name="acc%d_%d_%d" % (b, mt, c))
 
         nc.vector.memset(wsc[:].rearrange("p s m -> p (s m)").bitcast(I32), 0)
-        nc.vector.memset(warm[:], 0.0)
         nc.vector.memset(codes[:, 0:LEAD], 0)
         nc.vector.memset(xsc[:, 0:LEAD].bitcast(I32), 0)
-        nc.scalar.activation(out=warm_out[:], in_=warm[:], func=SIGMOID)
 
         def load(k):
             s, h = divmod(k, HALVES)
@@ -91,16 +87,18 @@ def tile_rows_glin_sigmoid_kernel(tc, x, w_words, w_scales, out):
                 in_=grouped[k][:, o:o + PIECE, :].rearrange("p n t -> p (n t)"),
             )
 
-        for k in range(CHUNKS):
+        def store(queue, k, mt):
             s, h = divmod(k, HALVES)
-            cols = slice(h * CHUNK, (h + 1) * CHUNK)
+            queue.dma_start(out=out_v[s, :, :, mt, h * CHUNK:(h + 1) * CHUNK], in_=res[k][:, :, mt, :])
+
+        for k in range(CHUNKS):
+            s = k // HALVES
             window = slice(k * CHUNK, k * CHUNK + WINDOW)
             for o in range(0, CHUNK, PIECE):
                 interleave(k, o)
             for o in range(0, CHUNK, PIECE):
                 quantise(k, o)
             for mt in range(M_TILES):
-                last = k == CHUNKS - 1 and mt == M_TILES - 1
                 for c in range(SIDE):
                     rows = slice(c * ROWS, (c + 1) * ROWS)
                     bank = acc[k % 2, mt, c]
@@ -114,7 +112,8 @@ def tile_rows_glin_sigmoid_kernel(tc, x, w_words, w_scales, out):
                         stop=True,
                     )
                     nc.scalar.activation(out=res[k][:, c, mt, :], in_=bank[:, LEAD:WINDOW], func=SIGMOID)
-                    if last:
-                        nc.sync.dma_start(out=out_v[s, :, c, mt, cols], in_=res[k][:, c, mt, :])
-                if not last:
-                    nc.sync.dma_start(out=out_v[s, :, :, mt, cols], in_=res[k][:, :, mt, :])
+                    if k >= 2 and mt == 0 and c == 0:
+                        store(nc.scalar, k - 1, 1)
+                if mt == 0 or k == 0:
+                    store(nc.sync, k, mt)
+        store(nc.scalar, CHUNKS - 1, 1)

@@ -21,20 +21,33 @@ SIDE = P // ROWS
 PAIRS = G // SIDE
 M_TILE = 128
 M_TILES = M // M_TILE
-CHUNK = 256
-HALVES = N // CHUNK
-CHUNKS = PAIRS * HALVES
-PIECE = 128
 WINDOW = 512
-LEAD = WINDOW - CHUNK
+BANKS = 4
+QUADRANT = 32
+SCALE_ROWS = 4
+RUN = 4
+WIDTHS = ((256, 256), (192, 192, 128))
+LEAD = WINDOW - WIDTHS[0][0]
+
+
+def first_piece(width):
+    cut = 1
+    while 2 * cut < width:
+        cut = 2 * cut
+    return cut
 
 
 def tile_rows_glin_sigmoid_kernel(tc, x, w_words, w_scales, out):
     nc = tc.nc
     x_v = x.rearrange("(s c) (p j) n -> s (c p) j n", c=SIDE, j=PACK)
     words_v = w_words.rearrange("(s c) p b -> (c p) s b", c=SIDE)
-    scales_v = w_scales.rearrange("(s c) (h r) m -> (c h) r s m", c=SIDE, r=4)
+    scales_v = w_scales.rearrange("(s c) (h r) m -> (c h) r s m", c=SIDE, r=SCALE_ROWS)
     out_v = out.rearrange("(s c) (t p) n -> s p c t n", c=SIDE, p=M_TILE)
+
+    chunks = []
+    for s in range(PAIRS):
+        for i in range(len(WIDTHS[s])):
+            chunks.append((s, sum(WIDTHS[s][:i]), WIDTHS[s][i]))
 
     with ExitStack() as ctx:
         sb = ctx.enter_context(tc.tile_pool(name="sb", bufs=1))
@@ -42,78 +55,75 @@ def tile_rows_glin_sigmoid_kernel(tc, x, w_words, w_scales, out):
         ctx.enter_context(tc.manual_schedule())
 
         words = sb.tile([P, PAIRS, 2 * M], U8, align_bytes=64, name="words")
-        wsc = sb.tile([P, PAIRS, M], U8, align_bytes=64, name="wsc")
-        codes = sb.tile([P, LEAD + CHUNKS * CHUNK], U32, align_bytes=64, name="codes")
-        xsc = sb.tile([P, LEAD + CHUNKS * CHUNK], U8, align_bytes=64, name="xsc")
+        w_plane = sb.tile([P, PAIRS, M], U8, align_bytes=64, name="w_plane")
+        codes = sb.tile([P, LEAD + PAIRS * N], U32, align_bytes=64, name="codes")
+        x_plane = sb.tile([P, LEAD + PAIRS * N], U8, align_bytes=64, name="x_plane")
         raw = []
         grouped = []
         res = []
-        for k in range(CHUNKS):
-            raw.append(sb.tile([P, PACK, CHUNK], F32, align_bytes=64, name="raw%d" % k))
-            grouped.append(sb.tile([P, CHUNK, PACK], BF16, align_bytes=64, name="grouped%d" % k))
-            res.append(sb.tile([P, SIDE, M_TILES, CHUNK], F32, align_bytes=64, name="res%d" % k))
+        for k, (s, first, width) in enumerate(chunks):
+            raw.append(sb.tile([P, PACK, width], F32, align_bytes=64, name="raw%d" % k))
+            grouped.append(sb.tile([P, width, PACK], BF16, align_bytes=64, name="grouped%d" % k))
+            res.append(sb.tile([P, SIDE, M_TILES, width], F32, align_bytes=64, name="res%d" % k))
         acc = {}
-        for b in range(2):
-            for mt in range(M_TILES):
-                for c in range(SIDE):
-                    acc[b, mt, c] = ps.tile([M_TILE, WINDOW], F32, name="acc%d_%d_%d" % (b, mt, c))
+        for b in range(BANKS):
+            for c in range(SIDE):
+                acc[b, c] = ps.tile([M_TILE, WINDOW], F32, name="acc%d_%d" % (b, c))
 
-        nc.vector.memset(wsc[:].rearrange("p s m -> p (s m)").bitcast(I32), 0)
+        nc.vector.memset(w_plane[:].rearrange("p s m -> p (s m)").bitcast(I32), 0)
         nc.vector.memset(codes[:, 0:LEAD], 0)
-        nc.vector.memset(xsc[:, 0:LEAD].bitcast(I32), 0)
+        nc.vector.memset(x_plane[:, 0:LEAD].bitcast(I32), 0)
 
         def load(k):
-            s, h = divmod(k, HALVES)
-            nc.sync.dma_start(out=raw[k][:], in_=x_v[s, :, :, h * CHUNK:(h + 1) * CHUNK])
+            s, first, width = chunks[k]
+            nc.sync.dma_start(out=raw[k][:], in_=x_v[s, :, :, first:first + width])
 
         load(0)
         nc.sync.dma_start(out=words[:].bitcast(I32), in_=words_v.bitcast(I32))
-        for q in range(4):
-            nc.sync.dma_start(out=wsc[32 * q:32 * q + 4, :, :].bitcast(I32), in_=scales_v[q].bitcast(I32))
-        for k in range(1, CHUNKS):
+        for q in range(P // QUADRANT):
+            nc.sync.dma_start(
+                out=w_plane[QUADRANT * q:QUADRANT * q + SCALE_ROWS, :, :].bitcast(I32),
+                in_=scales_v[q].bitcast(I32),
+            )
+        for k in range(1, len(chunks)):
             load(k)
 
-        def interleave(k, o):
+        def interleave(k, lo, hi):
             nc.vector.tensor_copy(
-                out=grouped[k][:, o:o + PIECE, :].rearrange("p (c i) t -> p c t i", i=4),
-                in_=raw[k][:, :, o:o + PIECE].rearrange("p t (c i) -> p c t i", i=4),
+                out=grouped[k][:, lo:hi, :].rearrange("p (c i) t -> p c t i", i=RUN),
+                in_=raw[k][:, :, lo:hi].rearrange("p t (c i) -> p c t i", i=RUN),
             )
 
-        def quantise(k, o):
-            c0 = LEAD + k * CHUNK + o
+        def quantise(k, lo, hi):
+            s, first, width = chunks[k]
+            base = LEAD + s * N + first
             nc.vector.quantize_mx(
-                out=codes[:, c0:c0 + PIECE].bitcast(FP8X4),
-                scales=xsc[:, c0:c0 + PIECE],
-                in_=grouped[k][:, o:o + PIECE, :].rearrange("p n t -> p (n t)"),
+                out=codes[:, base + lo:base + hi].bitcast(FP8X4),
+                scales=x_plane[:, base + lo:base + hi],
+                in_=grouped[k][:, lo:hi, :].rearrange("p n t -> p (n t)"),
             )
 
-        def store(queue, k, mt):
-            s, h = divmod(k, HALVES)
-            queue.dma_start(out=out_v[s, :, :, mt, h * CHUNK:(h + 1) * CHUNK], in_=res[k][:, :, mt, :])
-
-        for k in range(CHUNKS):
-            s = k // HALVES
-            window = slice(k * CHUNK, k * CHUNK + WINDOW)
-            for o in range(0, CHUNK, PIECE):
-                interleave(k, o)
-            for o in range(0, CHUNK, PIECE):
-                quantise(k, o)
+        for k, (s, first, width) in enumerate(chunks):
+            cut = first_piece(width)
+            pieces = ((0, cut), (cut, width))
+            for lo, hi in pieces:
+                interleave(k, lo, hi)
+            for lo, hi in pieces:
+                quantise(k, lo, hi)
+            end = LEAD + s * N + first + width
+            window = slice(end - WINDOW, end)
             for mt in range(M_TILES):
                 for c in range(SIDE):
                     rows = slice(c * ROWS, (c + 1) * ROWS)
-                    bank = acc[k % 2, mt, c]
+                    bank = acc[(k * M_TILES + mt) % BANKS, c]
                     nc.tensor.matmul_mx(
                         out=bank[:],
                         lhsT=words[rows, s, 2 * M_TILE * mt:2 * M_TILE * (mt + 1)].bitcast(FP4X4),
-                        lhsT_scale=wsc[rows, s, M_TILE * mt:M_TILE * (mt + 1)],
+                        lhsT_scale=w_plane[rows, s, M_TILE * mt:M_TILE * (mt + 1)],
                         rhs=codes[rows, window].bitcast(FP8X4),
-                        rhs_scale=xsc[rows, window],
+                        rhs_scale=x_plane[rows, window],
                         start=True,
                         stop=True,
                     )
-                    nc.scalar.activation(out=res[k][:, c, mt, :], in_=bank[:, LEAD:WINDOW], func=SIGMOID)
-                    if k >= 2 and mt == 0 and c == 0:
-                        store(nc.scalar, k - 1, 1)
-                if mt == 0 or k == 0:
-                    store(nc.sync, k, mt)
-        store(nc.scalar, CHUNKS - 1, 1)
+                    nc.scalar.activation(out=res[k][:, c, mt, :], in_=bank[:, WINDOW - width:WINDOW], func=SIGMOID)
+                nc.sync.dma_start(out=out_v[s, :, :, mt, first:first + width], in_=res[k][:, :, mt, :])

@@ -26,15 +26,11 @@ BANKS = 4
 QUADRANT = 32
 SCALE_ROWS = 4
 RUN = 4
-WIDTHS = ((256, 256), (192, 192, 128))
-LEAD = WINDOW - WIDTHS[0][0]
-
-
-def first_piece(width):
-    cut = 1
-    while 2 * cut < width:
-        cut = 2 * cut
-    return cut
+CHUNK = N // 2
+HALVES = N // CHUNK
+CHUNKS = PAIRS * HALVES
+PIECE = CHUNK // 2
+LEAD = WINDOW - CHUNK
 
 
 def tile_rows_glin_sigmoid_kernel(tc, x, w_words, w_scales, out):
@@ -43,11 +39,6 @@ def tile_rows_glin_sigmoid_kernel(tc, x, w_words, w_scales, out):
     words_v = w_words.rearrange("(s c) p b -> (c p) s b", c=SIDE)
     scales_v = w_scales.rearrange("(s c) (h r) m -> (c h) r s m", c=SIDE, r=SCALE_ROWS)
     out_v = out.rearrange("(s c) (t p) n -> s p c t n", c=SIDE, p=M_TILE)
-
-    chunks = []
-    for s in range(PAIRS):
-        for i in range(len(WIDTHS[s])):
-            chunks.append((s, sum(WIDTHS[s][:i]), WIDTHS[s][i]))
 
     with ExitStack() as ctx:
         sb = ctx.enter_context(tc.tile_pool(name="sb", bufs=1))
@@ -61,10 +52,10 @@ def tile_rows_glin_sigmoid_kernel(tc, x, w_words, w_scales, out):
         raw = []
         grouped = []
         res = []
-        for k, (s, first, width) in enumerate(chunks):
-            raw.append(sb.tile([P, PACK, width], F32, align_bytes=64, name="raw%d" % k))
-            grouped.append(sb.tile([P, width, PACK], BF16, align_bytes=64, name="grouped%d" % k))
-            res.append(sb.tile([P, SIDE, M_TILES, width], F32, align_bytes=64, name="res%d" % k))
+        for k in range(CHUNKS):
+            raw.append(sb.tile([P, PACK, CHUNK], F32, align_bytes=64, name="raw%d" % k))
+            grouped.append(sb.tile([P, CHUNK, PACK], BF16, align_bytes=64, name="grouped%d" % k))
+            res.append(sb.tile([P, SIDE, M_TILES, CHUNK], F32, align_bytes=64, name="res%d" % k))
         acc = {}
         for b in range(BANKS):
             for c in range(SIDE):
@@ -75,8 +66,8 @@ def tile_rows_glin_sigmoid_kernel(tc, x, w_words, w_scales, out):
         nc.vector.memset(x_plane[:, 0:LEAD].bitcast(I32), 0)
 
         def load(k):
-            s, first, width = chunks[k]
-            nc.sync.dma_start(out=raw[k][:], in_=x_v[s, :, :, first:first + width])
+            s, h = divmod(k, HALVES)
+            nc.sync.dma_start(out=raw[k][:], in_=x_v[s, :, :, h * CHUNK:(h + 1) * CHUNK])
 
         load(0)
         nc.sync.dma_start(out=words[:].bitcast(I32), in_=words_v.bitcast(I32))
@@ -85,33 +76,32 @@ def tile_rows_glin_sigmoid_kernel(tc, x, w_words, w_scales, out):
                 out=w_plane[QUADRANT * q:QUADRANT * q + SCALE_ROWS, :, :].bitcast(I32),
                 in_=scales_v[q].bitcast(I32),
             )
-        for k in range(1, len(chunks)):
+        for k in range(1, CHUNKS):
             load(k)
 
-        def interleave(k, lo, hi):
+        def interleave(k, lo):
             nc.vector.tensor_copy(
-                out=grouped[k][:, lo:hi, :].rearrange("p (c i) t -> p c t i", i=RUN),
-                in_=raw[k][:, :, lo:hi].rearrange("p t (c i) -> p c t i", i=RUN),
+                out=grouped[k][:, lo:lo + PIECE, :].rearrange("p (c i) t -> p c t i", i=RUN),
+                in_=raw[k][:, :, lo:lo + PIECE].rearrange("p t (c i) -> p c t i", i=RUN),
             )
 
-        def quantise(k, lo, hi):
-            s, first, width = chunks[k]
-            base = LEAD + s * N + first
+        def quantise(k, lo):
+            start = LEAD + k * CHUNK + lo
             nc.vector.quantize_mx(
-                out=codes[:, base + lo:base + hi].bitcast(FP8X4),
-                scales=x_plane[:, base + lo:base + hi],
-                in_=grouped[k][:, lo:hi, :].rearrange("p n t -> p (n t)"),
+                out=codes[:, start:start + PIECE].bitcast(FP8X4),
+                scales=x_plane[:, start:start + PIECE],
+                in_=grouped[k][:, lo:lo + PIECE, :].rearrange("p n t -> p (n t)"),
             )
 
-        for k, (s, first, width) in enumerate(chunks):
-            cut = first_piece(width)
-            pieces = ((0, cut), (cut, width))
-            for lo, hi in pieces:
-                interleave(k, lo, hi)
-            for lo, hi in pieces:
-                quantise(k, lo, hi)
-            end = LEAD + s * N + first + width
-            window = slice(end - WINDOW, end)
+        for k in range(CHUNKS):
+            s, h = divmod(k, HALVES)
+            cols = slice(h * CHUNK, (h + 1) * CHUNK)
+            window = slice(k * CHUNK, k * CHUNK + WINDOW)
+            for lo in range(0, CHUNK, PIECE):
+                interleave(k, lo)
+            for lo in range(0, CHUNK, PIECE):
+                quantise(k, lo)
+            last = k == CHUNKS - 1
             for mt in range(M_TILES):
                 for c in range(SIDE):
                     rows = slice(c * ROWS, (c + 1) * ROWS)
@@ -125,5 +115,8 @@ def tile_rows_glin_sigmoid_kernel(tc, x, w_words, w_scales, out):
                         start=True,
                         stop=True,
                     )
-                    nc.scalar.activation(out=res[k][:, c, mt, :], in_=bank[:, WINDOW - width:WINDOW], func=SIGMOID)
-                nc.sync.dma_start(out=out_v[s, :, :, mt, first:first + width], in_=res[k][:, :, mt, :])
+                    nc.scalar.activation(out=res[k][:, c, mt, :], in_=bank[:, LEAD:WINDOW], func=SIGMOID)
+                    if last:
+                        nc.sync.dma_start(out=out_v[s, :, c, mt, cols], in_=res[k][:, c, mt, :])
+                if not last:
+                    nc.sync.dma_start(out=out_v[s, :, :, mt, cols], in_=res[k][:, :, mt, :])

@@ -30,6 +30,7 @@ CHUNK = N // 2
 HALVES = N // CHUNK
 CHUNKS = PAIRS * HALVES
 PIECE = CHUNK // 2
+SPLIT = (1,)
 LEAD = WINDOW - CHUNK
 
 
@@ -45,15 +46,19 @@ def tile_rows_glin_sigmoid_kernel(tc, x, w_words, w_scales, out):
         ps = ctx.enter_context(tc.psum_pool(name="ps", bufs=1))
         ctx.enter_context(tc.manual_schedule())
 
-        words = sb.tile([P, PAIRS, 2 * M], U8, align_bytes=64, name="words")
+        words = []
+        for s in range(PAIRS):
+            words.append(sb.tile([P, 2 * M], U8, align_bytes=64, name="words%d" % s))
         w_plane = sb.tile([P, PAIRS, M], U8, align_bytes=64, name="w_plane")
         codes = sb.tile([P, LEAD + PAIRS * N], U32, align_bytes=64, name="codes")
         x_plane = sb.tile([P, LEAD + PAIRS * N], U8, align_bytes=64, name="x_plane")
-        raw = []
+        raw = {}
         grouped = []
         res = []
         for k in range(CHUNKS):
-            raw.append(sb.tile([P, PACK, CHUNK], F32, align_bytes=64, name="raw%d" % k))
+            width = PIECE if k in SPLIT else CHUNK
+            for lo in range(0, CHUNK, width):
+                raw[k, lo] = sb.tile([P, PACK, width], F32, align_bytes=64, name="raw%d_%d" % (k, lo))
             grouped.append(sb.tile([P, CHUNK, PACK], BF16, align_bytes=64, name="grouped%d" % k))
             res.append(sb.tile([P, SIDE, M_TILES, CHUNK], F32, align_bytes=64, name="res%d" % k))
         acc = {}
@@ -67,40 +72,50 @@ def tile_rows_glin_sigmoid_kernel(tc, x, w_words, w_scales, out):
 
         def load(k):
             s, h = divmod(k, HALVES)
-            nc.sync.dma_start(out=raw[k][:], in_=x_v[s, :, :, h * CHUNK:(h + 1) * CHUNK])
+            width = PIECE if k in SPLIT else CHUNK
+            for lo in range(0, CHUNK, width):
+                nc.sync.dma_start(out=raw[k, lo][:], in_=x_v[s, :, :, h * CHUNK + lo:h * CHUNK + lo + width])
+
+        def load_words(s):
+            nc.sync.dma_start(out=words[s][:].bitcast(I32), in_=words_v[:, s, :].bitcast(I32))
 
         load(0)
-        nc.sync.dma_start(out=words[:].bitcast(I32), in_=words_v.bitcast(I32))
+        load_words(0)
         for q in range(P // QUADRANT):
             nc.sync.dma_start(
                 out=w_plane[QUADRANT * q:QUADRANT * q + SCALE_ROWS, :, :].bitcast(I32),
                 in_=scales_v[q].bitcast(I32),
             )
-        for k in range(1, CHUNKS):
-            load(k)
+        load(1)
+        load(2)
+        load_words(1)
+        load(3)
 
-        def interleave(k, lo):
+        def interleave(k, lo, n):
+            base = lo // PIECE * PIECE if k in SPLIT else 0
             nc.vector.tensor_copy(
-                out=grouped[k][:, lo:lo + PIECE, :].rearrange("p (c i) t -> p c t i", i=RUN),
-                in_=raw[k][:, :, lo:lo + PIECE].rearrange("p t (c i) -> p c t i", i=RUN),
+                out=grouped[k][:, lo:lo + n, :].rearrange("p (c i) t -> p c t i", i=RUN),
+                in_=raw[k, base][:, :, lo - base:lo - base + n].rearrange("p t (c i) -> p c t i", i=RUN),
             )
 
-        def quantise(k, lo):
+        def quantise(k, lo, n):
             start = LEAD + k * CHUNK + lo
             nc.vector.quantize_mx(
-                out=codes[:, start:start + PIECE].bitcast(FP8X4),
-                scales=x_plane[:, start:start + PIECE],
-                in_=grouped[k][:, lo:lo + PIECE, :].rearrange("p n t -> p (n t)"),
+                out=codes[:, start:start + n].bitcast(FP8X4),
+                scales=x_plane[:, start:start + n],
+                in_=grouped[k][:, lo:lo + n, :].rearrange("p n t -> p (n t)"),
             )
 
         for k in range(CHUNKS):
             s, h = divmod(k, HALVES)
             cols = slice(h * CHUNK, (h + 1) * CHUNK)
             window = slice(k * CHUNK, k * CHUNK + WINDOW)
-            for lo in range(0, CHUNK, PIECE):
-                interleave(k, lo)
-            for lo in range(0, CHUNK, PIECE):
-                quantise(k, lo)
+            width = PIECE if k in SPLIT else CHUNK
+            for first in range(0, CHUNK, width):
+                for lo in range(first, first + width, width // 2):
+                    interleave(k, lo, width // 2)
+                for lo in range(first, first + width, width // 2):
+                    quantise(k, lo, width // 2)
             last = k == CHUNKS - 1
             for mt in range(M_TILES):
                 for c in range(SIDE):
@@ -108,7 +123,7 @@ def tile_rows_glin_sigmoid_kernel(tc, x, w_words, w_scales, out):
                     bank = acc[(k * M_TILES + mt) % BANKS, c]
                     nc.tensor.matmul_mx(
                         out=bank[:],
-                        lhsT=words[rows, s, 2 * M_TILE * mt:2 * M_TILE * (mt + 1)].bitcast(FP4X4),
+                        lhsT=words[s][rows, 2 * M_TILE * mt:2 * M_TILE * (mt + 1)].bitcast(FP4X4),
                         lhsT_scale=w_plane[rows, s, M_TILE * mt:M_TILE * (mt + 1)],
                         rhs=codes[rows, window].bitcast(FP8X4),
                         rhs_scale=x_plane[rows, window],

@@ -25,7 +25,7 @@ WINDOW = 512
 BANKS = 4
 QUADRANT = 32
 SCALE_ROWS = 4
-RUN = 4
+RUN = 2
 CHUNK = N // 2
 HALVES = N // CHUNK
 CHUNKS = PAIRS * HALVES

@@ -25,6 +25,7 @@ WINDOW = 512
 BANKS = 4
 QUADRANT = 32
 SCALE_ROWS = 4
+ALIGN = 256
 RUN = 2
 CHUNK = N // 2
 HALVES = N // CHUNK
@@ -48,19 +49,19 @@ def tile_rows_glin_sigmoid_kernel(tc, x, w_words, w_scales, out):
 
         words = []
         for s in range(PAIRS):
-            words.append(sb.tile([P, 2 * M], U8, align_bytes=64, name="words%d" % s))
-        w_plane = sb.tile([P, PAIRS, M], U8, align_bytes=64, name="w_plane")
-        codes = sb.tile([P, LEAD + PAIRS * N], U32, align_bytes=64, name="codes")
-        x_plane = sb.tile([P, LEAD + PAIRS * N], U8, align_bytes=64, name="x_plane")
+            words.append(sb.tile([P, 2 * M], U8, align_bytes=ALIGN, name="words%d" % s))
+        w_plane = sb.tile([P, PAIRS, M], U8, align_bytes=ALIGN, name="w_plane")
+        codes = sb.tile([P, LEAD + PAIRS * N], U32, align_bytes=ALIGN, name="codes")
+        x_plane = sb.tile([P, LEAD + PAIRS * N], U8, align_bytes=ALIGN, name="x_plane")
         raw = {}
         grouped = []
         res = []
         for k in range(CHUNKS):
             width = PIECE if k in SPLIT else CHUNK
             for lo in range(0, CHUNK, width):
-                raw[k, lo] = sb.tile([P, PACK, width], F32, align_bytes=64, name="raw%d_%d" % (k, lo))
-            grouped.append(sb.tile([P, CHUNK, PACK], BF16, align_bytes=64, name="grouped%d" % k))
-            res.append(sb.tile([P, SIDE, M_TILES, CHUNK], F32, align_bytes=64, name="res%d" % k))
+                raw[k, lo] = sb.tile([P, PACK, width], F32, align_bytes=ALIGN, name="raw%d_%d" % (k, lo))
+            grouped.append(sb.tile([P, CHUNK, PACK], BF16, align_bytes=ALIGN, name="grouped%d" % k))
+            res.append(sb.tile([P, SIDE, M_TILES, CHUNK], F32, align_bytes=ALIGN, name="res%d" % k))
         acc = {}
         for b in range(BANKS):
             for c in range(SIDE):

@@ -27,12 +27,12 @@ QUADRANT = 32
 SCALE_ROWS = 4
 ALIGN = 256
 RUN = 2
-CHUNK = N // 2
-HALVES = N // CHUNK
-CHUNKS = PAIRS * HALVES
-PIECE = CHUNK // 2
-SPLIT = (1,)
-LEAD = WINDOW - CHUNK
+LOADS = ((256,),(128,128,),(128,128,),(128,128,),)
+PIECES = (128,64,64,64,)
+STORES = ("mt","mt","mt","one",)
+WIDTHS = [sum(loads) for loads in LOADS]
+STARTS = [sum(WIDTHS[:k]) for k in range(len(WIDTHS))]
+LEAD = WINDOW - WIDTHS[0]
 
 
 def tile_rows_glin_sigmoid_kernel(tc, x, w_words, w_scales, out):
@@ -53,15 +53,16 @@ def tile_rows_glin_sigmoid_kernel(tc, x, w_words, w_scales, out):
         w_plane = sb.tile([P, PAIRS, M], U8, align_bytes=ALIGN, name="w_plane")
         codes = sb.tile([P, LEAD + PAIRS * N], U32, align_bytes=ALIGN, name="codes")
         x_plane = sb.tile([P, LEAD + PAIRS * N], U8, align_bytes=ALIGN, name="x_plane")
-        raw = {}
+        raw = []
         grouped = []
         res = []
-        for k in range(CHUNKS):
-            width = PIECE if k in SPLIT else CHUNK
-            for lo in range(0, CHUNK, width):
-                raw[k, lo] = sb.tile([P, PACK, width], F32, align_bytes=ALIGN, name="raw%d_%d" % (k, lo))
-            grouped.append(sb.tile([P, CHUNK, PACK], BF16, align_bytes=ALIGN, name="grouped%d" % k))
-            res.append(sb.tile([P, SIDE, M_TILES, CHUNK], F32, align_bytes=ALIGN, name="res%d" % k))
+        for k, width in enumerate(WIDTHS):
+            lo = STARTS[k]
+            for w in LOADS[k]:
+                raw.append((k, lo, w, sb.tile([P, PACK, w], F32, align_bytes=ALIGN, name="raw%d" % lo)))
+                lo = lo + w
+            grouped.append(sb.tile([P, width, PACK], BF16, align_bytes=ALIGN, name="grouped%d" % k))
+            res.append(sb.tile([P, SIDE, M_TILES, width], F32, align_bytes=ALIGN, name="res%d" % k))
         acc = {}
         for b in range(BANKS):
             for c in range(SIDE):
@@ -71,68 +72,71 @@ def tile_rows_glin_sigmoid_kernel(tc, x, w_words, w_scales, out):
         nc.vector.memset(codes[:, 0:LEAD], 0)
         nc.vector.memset(x_plane[:, 0:LEAD].bitcast(I32), 0)
 
-        def load(k):
-            s, h = divmod(k, HALVES)
-            width = PIECE if k in SPLIT else CHUNK
-            for lo in range(0, CHUNK, width):
-                nc.sync.dma_start(out=raw[k, lo][:], in_=x_v[s, :, :, h * CHUNK + lo:h * CHUNK + lo + width])
+        def load_scales():
+            for q in range(P // QUADRANT):
+                nc.sync.dma_start(
+                    out=w_plane[QUADRANT * q:QUADRANT * q + SCALE_ROWS, :, :].bitcast(I32),
+                    in_=scales_v[q].bitcast(I32),
+                )
 
-        def load_words(s):
-            nc.sync.dma_start(out=words[s][:].bitcast(I32), in_=words_v[:, s, :].bitcast(I32))
+        for i, (k, lo, w, tile) in enumerate(raw):
+            nc.sync.dma_start(out=tile[:], in_=x_v[lo // N, :, :, lo % N:lo % N + w])
+            if i == 0:
+                nc.sync.dma_start(out=words[0][:].bitcast(I32), in_=words_v[:, 0, :].bitcast(I32))
+                load_scales()
+            if i == 4:
+                nc.sync.dma_start(out=words[1][:].bitcast(I32), in_=words_v[:, 1, :].bitcast(I32))
 
-        load(0)
-        load_words(0)
-        for q in range(P // QUADRANT):
-            nc.sync.dma_start(
-                out=w_plane[QUADRANT * q:QUADRANT * q + SCALE_ROWS, :, :].bitcast(I32),
-                in_=scales_v[q].bitcast(I32),
-            )
-        load(1)
-        load(2)
-        load_words(1)
-        load(3)
-
-        def interleave(k, lo, n):
-            base = lo // PIECE * PIECE if k in SPLIT else 0
+        def interleave(k, tile, base, lo, n):
             nc.vector.tensor_copy(
-                out=grouped[k][:, lo:lo + n, :].rearrange("p (c i) t -> p c t i", i=RUN),
-                in_=raw[k, base][:, :, lo - base:lo - base + n].rearrange("p t (c i) -> p c t i", i=RUN),
+                out=grouped[k][:, lo - STARTS[k]:lo - STARTS[k] + n, :].rearrange("p (c i) t -> p c t i", i=RUN),
+                in_=tile[:, :, lo - base:lo - base + n].rearrange("p t (c i) -> p c t i", i=RUN),
             )
 
         def quantise(k, lo, n):
-            start = LEAD + k * CHUNK + lo
             nc.vector.quantize_mx(
-                out=codes[:, start:start + n].bitcast(FP8X4),
-                scales=x_plane[:, start:start + n],
-                in_=grouped[k][:, lo:lo + n, :].rearrange("p n t -> p (n t)"),
+                out=codes[:, LEAD + lo:LEAD + lo + n].bitcast(FP8X4),
+                scales=x_plane[:, LEAD + lo:LEAD + lo + n],
+                in_=grouped[k][:, lo - STARTS[k]:lo - STARTS[k] + n, :].rearrange("p n t -> p (n t)"),
             )
 
-        for k in range(CHUNKS):
-            s, h = divmod(k, HALVES)
-            cols = slice(h * CHUNK, (h + 1) * CHUNK)
-            window = slice(k * CHUNK, k * CHUNK + WINDOW)
-            width = PIECE if k in SPLIT else CHUNK
-            for first in range(0, CHUNK, width):
-                for lo in range(first, first + width, width // 2):
-                    interleave(k, lo, width // 2)
-                for lo in range(first, first + width, width // 2):
-                    quantise(k, lo, width // 2)
-            last = k == CHUNKS - 1
+        def multiply(k, mt, c):
+            s = STARTS[k] // N
+            end = LEAD + STARTS[k] + WIDTHS[k]
+            window = slice(end - WINDOW, end)
+            rows = slice(c * ROWS, (c + 1) * ROWS)
+            nc.tensor.matmul_mx(
+                out=acc[(k * M_TILES + mt) % BANKS, c][:],
+                lhsT=words[s][rows, 2 * M_TILE * mt:2 * M_TILE * (mt + 1)].bitcast(FP4X4),
+                lhsT_scale=w_plane[rows, s, M_TILE * mt:M_TILE * (mt + 1)],
+                rhs=codes[rows, window].bitcast(FP8X4),
+                rhs_scale=x_plane[rows, window],
+                start=True,
+                stop=True,
+            )
+
+        for k, width in enumerate(WIDTHS):
+            s = STARTS[k] // N
+            cols = slice(STARTS[k] % N, STARTS[k] % N + width)
+            for owner, base, w, tile in raw:
+                if owner == k:
+                    cuts = [(lo, min(PIECES[k], base + w - lo)) for lo in range(base, base + w, PIECES[k])]
+                    for lo, n in cuts:
+                        interleave(k, tile, base, lo, n)
+                    for lo, n in cuts:
+                        quantise(k, lo, n)
             for mt in range(M_TILES):
                 for c in range(SIDE):
-                    rows = slice(c * ROWS, (c + 1) * ROWS)
+                    multiply(k, mt, c)
+                for c in range(SIDE):
                     bank = acc[(k * M_TILES + mt) % BANKS, c]
-                    nc.tensor.matmul_mx(
-                        out=bank[:],
-                        lhsT=words[s][rows, 2 * M_TILE * mt:2 * M_TILE * (mt + 1)].bitcast(FP4X4),
-                        lhsT_scale=w_plane[rows, s, M_TILE * mt:M_TILE * (mt + 1)],
-                        rhs=codes[rows, window].bitcast(FP8X4),
-                        rhs_scale=x_plane[rows, window],
-                        start=True,
-                        stop=True,
-                    )
-                    nc.scalar.activation(out=res[k][:, c, mt, :], in_=bank[:, LEAD:WINDOW], func=SIGMOID)
-                    if last:
+                    nc.scalar.activation(out=res[k][:, c, mt, :], in_=bank[:, WINDOW - width:WINDOW], func=SIGMOID)
+                    if STORES[k] == "one":
                         nc.sync.dma_start(out=out_v[s, :, c, mt, cols], in_=res[k][:, c, mt, :])
-                if not last:
+                if STORES[k] == "mt":
                     nc.sync.dma_start(out=out_v[s, :, :, mt, cols], in_=res[k][:, :, mt, :])
+            if STORES[k] == "all":
+                nc.sync.dma_start(
+                    out=out_v[s, :, :, :, cols].rearrange("p c t n -> p (c t) n"),
+                    in_=res[k][:].rearrange("p c t n -> p (c t) n"),
+                )

@@ -29,7 +29,7 @@ ALIGN = 256
 RUN = 2
 LOADS = ((256,),(128,128,),(128,128,),(128,128,),)
 PIECES = (128,64,64,64,)
-STORES = ("mt","mt","mt","one",)
+STORES = ("mt","mt","mt","mt",)
 WIDTHS = [sum(loads) for loads in LOADS]
 STARTS = [sum(WIDTHS[:k]) for k in range(len(WIDTHS))]
 LEAD = WINDOW - WIDTHS[0]

@@ -27,12 +27,11 @@ QUADRANT = 32
 SCALE_ROWS = 4
 ALIGN = 256
 RUN = 2
-LOADS = ((256,),(128,128,),(128,128,),(128,128,),)
-PIECES = (128,64,64,64,)
-STORES = ("mt","mt","mt","mt",)
-WIDTHS = [sum(loads) for loads in LOADS]
-STARTS = [sum(WIDTHS[:k]) for k in range(len(WIDTHS))]
-LEAD = WINDOW - WIDTHS[0]
+CHUNK = 256
+CHUNKS = PAIRS * N // CHUNK
+LEAD = WINDOW - CHUNK
+LOADS = (128, 128)
+PIECES = (128, 64, 64)
 
 
 def tile_rows_glin_sigmoid_kernel(tc, x, w_words, w_scales, out):
@@ -56,57 +55,77 @@ def tile_rows_glin_sigmoid_kernel(tc, x, w_words, w_scales, out):
         raw = []
         grouped = []
         res = []
-        for k, width in enumerate(WIDTHS):
-            lo = STARTS[k]
-            for w in LOADS[k]:
-                raw.append((k, lo, w, sb.tile([P, PACK, w], F32, align_bytes=ALIGN, name="raw%d" % lo)))
-                lo = lo + w
-            grouped.append(sb.tile([P, width, PACK], BF16, align_bytes=ALIGN, name="grouped%d" % k))
-            res.append(sb.tile([P, SIDE, M_TILES, width], F32, align_bytes=ALIGN, name="res%d" % k))
+        for k in range(CHUNKS):
+            for i, width in enumerate(LOADS):
+                first = k * CHUNK + sum(LOADS[:i])
+                tile = sb.tile([P, PACK, width], F32, align_bytes=ALIGN, name="raw%d" % first)
+                raw.append((first, width, tile))
+            grouped.append(sb.tile([P, CHUNK, PACK], BF16, align_bytes=ALIGN, name="grouped%d" % k))
+            res.append(sb.tile([P, SIDE, M_TILES, CHUNK], F32, align_bytes=ALIGN, name="res%d" % k))
         acc = {}
         for b in range(BANKS):
             for c in range(SIDE):
-                acc[b, c] = ps.tile([M_TILE, WINDOW], F32, name="acc%d_%d" % (b, c))
+                acc[c, b] = ps.tile([M_TILE, WINDOW], F32, name="acc%d_%d" % (b, c))
+        used = [[] for c in range(SIDE)]
 
         nc.vector.memset(w_plane[:].rearrange("p s m -> p (s m)").bitcast(I32), 0)
         nc.vector.memset(codes[:, 0:LEAD], 0)
         nc.vector.memset(x_plane[:, 0:LEAD].bitcast(I32), 0)
 
-        def load_scales():
-            for q in range(P // QUADRANT):
-                nc.sync.dma_start(
-                    out=w_plane[QUADRANT * q:QUADRANT * q + SCALE_ROWS, :, :].bitcast(I32),
-                    in_=scales_v[q].bitcast(I32),
-                )
+        def load_chunk(k):
+            for first, width, tile in raw:
+                if first // CHUNK == k:
+                    nc.sync.dma_start(out=tile[:], in_=x_v[first // N, :, :, first % N:first % N + width])
 
-        for i, (k, lo, w, tile) in enumerate(raw):
-            nc.sync.dma_start(out=tile[:], in_=x_v[lo // N, :, :, lo % N:lo % N + w])
-            if i == 0:
-                nc.sync.dma_start(out=words[0][:].bitcast(I32), in_=words_v[:, 0, :].bitcast(I32))
-                load_scales()
-            if i == 4:
-                nc.sync.dma_start(out=words[1][:].bitcast(I32), in_=words_v[:, 1, :].bitcast(I32))
+        def load_words(s):
+            nc.sync.dma_start(out=words[s][:].bitcast(I32), in_=words_v[:, s, :].bitcast(I32))
 
-        def interleave(k, tile, base, lo, n):
-            nc.vector.tensor_copy(
-                out=grouped[k][:, lo - STARTS[k]:lo - STARTS[k] + n, :].rearrange("p (c i) t -> p c t i", i=RUN),
-                in_=tile[:, :, lo - base:lo - base + n].rearrange("p t (c i) -> p c t i", i=RUN),
+        def load_scales(q):
+            nc.sync.dma_start(
+                out=w_plane[QUADRANT * q:QUADRANT * q + SCALE_ROWS, :, :].bitcast(I32),
+                in_=scales_v[q].bitcast(I32),
             )
 
-        def quantise(k, lo, n):
+        load_chunk(0)
+        load_words(0)
+        for q in range(P // QUADRANT):
+            load_scales(q)
+        load_chunk(1)
+        load_chunk(2)
+        load_words(1)
+        load_chunk(3)
+
+        def interleave(lo, n):
+            for first, width, tile in raw:
+                if first <= lo < first + width:
+                    nc.vector.tensor_copy(
+                        out=grouped[lo // CHUNK][:, lo % CHUNK:lo % CHUNK + n, :].rearrange("p (c i) t -> p c t i", i=RUN),
+                        in_=tile[:, :, lo - first:lo - first + n].rearrange("p t (c i) -> p c t i", i=RUN),
+                    )
+
+        def quantise(lo, n):
+            cols = slice(LEAD + lo, LEAD + lo + n)
             nc.vector.quantize_mx(
-                out=codes[:, LEAD + lo:LEAD + lo + n].bitcast(FP8X4),
-                scales=x_plane[:, LEAD + lo:LEAD + lo + n],
-                in_=grouped[k][:, lo - STARTS[k]:lo - STARTS[k] + n, :].rearrange("p n t -> p (n t)"),
+                out=codes[:, cols].bitcast(FP8X4),
+                scales=x_plane[:, cols],
+                in_=grouped[lo // CHUNK][:, lo % CHUNK:lo % CHUNK + n, :].rearrange("p n t -> p (n t)"),
             )
 
-        def multiply(k, mt, c):
-            s = STARTS[k] // N
-            end = LEAD + STARTS[k] + WIDTHS[k]
-            window = slice(end - WINDOW, end)
+        def prepare(lo, pieces):
+            cuts = [(lo + sum(pieces[:i]), n) for i, n in enumerate(pieces)]
+            for start, n in cuts:
+                interleave(start, n)
+            for start, n in cuts:
+                quantise(start, n)
+
+        def multiply(lo, n, mt, c):
+            s = lo // N
+            window = slice(LEAD + lo + n - WINDOW, LEAD + lo + n)
             rows = slice(c * ROWS, (c + 1) * ROWS)
+            bank = acc[c, len(used[c]) % BANKS]
+            used[c].append(bank)
             nc.tensor.matmul_mx(
-                out=acc[(k * M_TILES + mt) % BANKS, c][:],
+                out=bank[:],
                 lhsT=words[s][rows, 2 * M_TILE * mt:2 * M_TILE * (mt + 1)].bitcast(FP4X4),
                 lhsT_scale=w_plane[rows, s, M_TILE * mt:M_TILE * (mt + 1)],
                 rhs=codes[rows, window].bitcast(FP8X4),
@@ -114,29 +133,27 @@ def tile_rows_glin_sigmoid_kernel(tc, x, w_words, w_scales, out):
                 start=True,
                 stop=True,
             )
+            nc.scalar.activation(
+                out=res[lo // CHUNK][:, c, mt, lo % CHUNK:lo % CHUNK + n],
+                in_=bank[:, WINDOW - n:WINDOW],
+                func=SIGMOID,
+            )
 
-        for k, width in enumerate(WIDTHS):
-            s = STARTS[k] // N
-            cols = slice(STARTS[k] % N, STARTS[k] % N + width)
-            for owner, base, w, tile in raw:
-                if owner == k:
-                    cuts = [(lo, min(PIECES[k], base + w - lo)) for lo in range(base, base + w, PIECES[k])]
-                    for lo, n in cuts:
-                        interleave(k, tile, base, lo, n)
-                    for lo, n in cuts:
-                        quantise(k, lo, n)
+        def store_tile(k, mt):
+            first = k * CHUNK % N
+            nc.sync.dma_start(out=out_v[k * CHUNK // N, :, :, mt, first:first + CHUNK], in_=res[k][:, :, mt, :])
+
+        def store_one(k, mt, c):
+            first = k * CHUNK % N
+            nc.sync.dma_start(out=out_v[k * CHUNK // N, :, c, mt, first:first + CHUNK], in_=res[k][:, c, mt, :])
+
+        for k in range(CHUNKS):
+            lo = k * CHUNK
+            prepare(lo, PIECES)
             for mt in range(M_TILES):
                 for c in range(SIDE):
-                    multiply(k, mt, c)
-                for c in range(SIDE):
-                    bank = acc[(k * M_TILES + mt) % BANKS, c]
-                    nc.scalar.activation(out=res[k][:, c, mt, :], in_=bank[:, WINDOW - width:WINDOW], func=SIGMOID)
-                    if STORES[k] == "one":
-                        nc.sync.dma_start(out=out_v[s, :, c, mt, cols], in_=res[k][:, c, mt, :])
-                if STORES[k] == "mt":
-                    nc.sync.dma_start(out=out_v[s, :, :, mt, cols], in_=res[k][:, :, mt, :])
-            if STORES[k] == "all":
-                nc.sync.dma_start(
-                    out=out_v[s, :, :, :, cols].rearrange("p c t n -> p (c t) n"),
-                    in_=res[k][:].rearrange("p c t n -> p (c t) n"),
-                )
+                    multiply(lo, CHUNK, mt, c)
+                    if k == CHUNKS - 1:
+                        store_one(k, mt, c)
+                if k < CHUNKS - 1:
+                    store_tile(k, mt)

@@ -31,6 +31,7 @@ CHUNK = 256
 CHUNKS = PAIRS * N // CHUNK
 LEAD = WINDOW - CHUNK
 LOADS = (128, 128)
+HALF_WORD = 2
 PIECES = (128, 64, 64)
 
 
@@ -56,12 +57,15 @@ def tile_rows_glin_sigmoid_kernel(tc, x, w_words, w_scales, out):
         grouped = []
         res = []
         for k in range(CHUNKS):
-            for i, width in enumerate(LOADS):
+            for i, width in enumerate(LOADS if k > 0 else ()):
                 first = k * CHUNK + sum(LOADS[:i])
                 tile = sb.tile([P, PACK, width], F32, align_bytes=ALIGN, name="raw%d" % first)
                 raw.append((first, width, tile))
             grouped.append(sb.tile([P, CHUNK, PACK], BF16, align_bytes=ALIGN, name="grouped%d" % k))
             res.append(sb.tile([P, SIDE, M_TILES, CHUNK], F32, align_bytes=ALIGN, name="res%d" % k))
+        head = []
+        for h in range(PACK // HALF_WORD):
+            head.append(sb.tile([P, HALF_WORD, CHUNK], F32, align_bytes=ALIGN, name="head%d" % h))
         acc = {}
         for b in range(BANKS):
             for c in range(SIDE):
@@ -86,7 +90,8 @@ def tile_rows_glin_sigmoid_kernel(tc, x, w_words, w_scales, out):
                 in_=scales_v[q].bitcast(I32),
             )
 
-        load_chunk(0)
+        for h, tile in enumerate(head):
+            nc.sync.dma_start(out=tile[:], in_=x_v[0, :, HALF_WORD * h:HALF_WORD * (h + 1), 0:CHUNK])
         load_words(0)
         for q in range(P // QUADRANT):
             load_scales(q)
@@ -111,10 +116,21 @@ def tile_rows_glin_sigmoid_kernel(tc, x, w_words, w_scales, out):
                 in_=grouped[lo // CHUNK][:, lo % CHUNK:lo % CHUNK + n, :].rearrange("p n t -> p (n t)"),
             )
 
+        def interleave_head(h, lo, n):
+            nc.vector.tensor_copy(
+                out=grouped[0][:, lo:lo + n, HALF_WORD * h:HALF_WORD * (h + 1)],
+                in_=head[h][:, :, lo:lo + n].rearrange("p t n -> p n t"),
+            )
+
         def prepare(lo, pieces):
             cuts = [(lo + sum(pieces[:i]), n) for i, n in enumerate(pieces)]
+            if lo == 0:
+                interleave_head(0, 0, CHUNK)
             for start, n in cuts:
-                interleave(start, n)
+                if lo == 0:
+                    interleave_head(1, start, n)
+                else:
+                    interleave(start, n)
             for start, n in cuts:
                 quantise(start, n)
 

@@ -31,7 +31,7 @@ CHUNK = 256
 CHUNKS = PAIRS * N // CHUNK
 LEAD = WINDOW - CHUNK
 LOADS = (128, 128)
-HALF_WORD = 2
+SINGLE = ((1, 0), (3, 0), (3, 1))
 PIECES = (128, 64, 64)
 
 
@@ -57,15 +57,12 @@ def tile_rows_glin_sigmoid_kernel(tc, x, w_words, w_scales, out):
         grouped = []
         res = []
         for k in range(CHUNKS):
-            for i, width in enumerate(LOADS if k > 0 else ()):
+            for i, width in enumerate(LOADS if k > 0 else (CHUNK,)):
                 first = k * CHUNK + sum(LOADS[:i])
                 tile = sb.tile([P, PACK, width], F32, align_bytes=ALIGN, name="raw%d" % first)
                 raw.append((first, width, tile))
             grouped.append(sb.tile([P, CHUNK, PACK], BF16, align_bytes=ALIGN, name="grouped%d" % k))
             res.append(sb.tile([P, SIDE, M_TILES, CHUNK], F32, align_bytes=ALIGN, name="res%d" % k))
-        head = []
-        for h in range(PACK // HALF_WORD):
-            head.append(sb.tile([P, HALF_WORD, CHUNK], F32, align_bytes=ALIGN, name="head%d" % h))
         acc = {}
         for b in range(BANKS):
             for c in range(SIDE):
@@ -90,8 +87,7 @@ def tile_rows_glin_sigmoid_kernel(tc, x, w_words, w_scales, out):
                 in_=scales_v[q].bitcast(I32),
             )
 
-        for h, tile in enumerate(head):
-            nc.sync.dma_start(out=tile[:], in_=x_v[0, :, HALF_WORD * h:HALF_WORD * (h + 1), 0:CHUNK])
+        load_chunk(0)
         load_words(0)
         for q in range(P // QUADRANT):
             load_scales(q)
@@ -116,21 +112,10 @@ def tile_rows_glin_sigmoid_kernel(tc, x, w_words, w_scales, out):
                 in_=grouped[lo // CHUNK][:, lo % CHUNK:lo % CHUNK + n, :].rearrange("p n t -> p (n t)"),
             )
 
-        def interleave_head(h, lo, n):
-            nc.vector.tensor_copy(
-                out=grouped[0][:, lo:lo + n, HALF_WORD * h:HALF_WORD * (h + 1)],
-                in_=head[h][:, :, lo:lo + n].rearrange("p t n -> p n t"),
-            )
-
         def prepare(lo, pieces):
             cuts = [(lo + sum(pieces[:i]), n) for i, n in enumerate(pieces)]
-            if lo == 0:
-                interleave_head(0, 0, CHUNK)
             for start, n in cuts:
-                if lo == 0:
-                    interleave_head(1, start, n)
-                else:
-                    interleave(start, n)
+                interleave(start, n)
             for start, n in cuts:
                 quantise(start, n)
 
@@ -169,7 +154,7 @@ def tile_rows_glin_sigmoid_kernel(tc, x, w_words, w_scales, out):
             for mt in range(M_TILES):
                 for c in range(SIDE):
                     multiply(lo, CHUNK, mt, c)
-                    if k == CHUNKS - 1:
+                    if (k, mt) in SINGLE:
                         store_one(k, mt, c)
-                if k < CHUNKS - 1:
+                if (k, mt) not in SINGLE:
                     store_tile(k, mt)

@@ -31,6 +31,8 @@ CHUNK = 256
 CHUNKS = PAIRS * N // CHUNK
 LEAD = WINDOW - CHUNK
 LOADS = (128, 128)
+FIRST_PIECES = (64, 64, 64, 64)
+SCALAR_PIECE = 128
 SINGLE = ((1, 0), (3, 0), (3, 1))
 PIECES = (128, 64, 64)
 
@@ -70,6 +72,9 @@ def tile_rows_glin_sigmoid_kernel(tc, x, w_words, w_scales, out):
         used = [[] for c in range(SIDE)]
 
         nc.vector.memset(w_plane[:].rearrange("p s m -> p (s m)").bitcast(I32), 0)
+        warm = sb.tile([P, 2], F32, align_bytes=ALIGN, name="warm")
+        nc.vector.memset(warm[:, 0:1], 0.0)
+        nc.scalar.activation(out=warm[:, 1:2], in_=warm[:, 0:1], func=SIGMOID)
         nc.vector.memset(codes[:, 0:LEAD], 0)
         nc.vector.memset(x_plane[:, 0:LEAD].bitcast(I32), 0)
 
@@ -96,10 +101,10 @@ def tile_rows_glin_sigmoid_kernel(tc, x, w_words, w_scales, out):
         load_words(1)
         load_chunk(3)
 
-        def interleave(lo, n):
+        def interleave(lo, n, copy):
             for first, width, tile in raw:
                 if first <= lo < first + width:
-                    nc.vector.tensor_copy(
+                    copy(
                         out=grouped[lo // CHUNK][:, lo % CHUNK:lo % CHUNK + n, :].rearrange("p (c i) t -> p c t i", i=RUN),
                         in_=tile[:, :, lo - first:lo - first + n].rearrange("p t (c i) -> p c t i", i=RUN),
                     )
@@ -115,7 +120,7 @@ def tile_rows_glin_sigmoid_kernel(tc, x, w_words, w_scales, out):
         def prepare(lo, pieces):
             cuts = [(lo + sum(pieces[:i]), n) for i, n in enumerate(pieces)]
             for start, n in cuts:
-                interleave(start, n)
+                interleave(start, n, nc.scalar.copy if start == SCALAR_PIECE else nc.vector.tensor_copy)
             for start, n in cuts:
                 quantise(start, n)
 
@@ -150,7 +155,7 @@ def tile_rows_glin_sigmoid_kernel(tc, x, w_words, w_scales, out):
 
         for k in range(CHUNKS):
             lo = k * CHUNK
-            prepare(lo, PIECES)
+            prepare(lo, PIECES if k > 0 else FIRST_PIECES)
             for mt in range(M_TILES):
                 for c in range(SIDE):
                     multiply(lo, CHUNK, mt, c)

from contextlib import ExitStack

import concourse.mybir as mybir

G, D, M, N = 4, 256, 256, 512
FLOPS = 2 * G * D * M * N

F32 = mybir.dt.float32
BF16 = mybir.dt.bfloat16
I32 = mybir.dt.int32
U32 = mybir.dt.uint32
U8 = mybir.dt.uint8
FP8X4 = mybir.dt.float8_e4m3fn_x4
FP4X4 = mybir.dt.float4_e2m1fn_x4
SIGMOID = mybir.ActivationFunctionType.Sigmoid

P = 128
PACK = 4
ROWS = D // PACK
SIDE = P // ROWS
PAIRS = G // SIDE
M_TILE = 128
M_TILES = M // M_TILE
WINDOW = 512
BANKS = 4
QUADRANT = 32
SCALE_ROWS = 4
ALIGN = 256
RUN = 2
CHUNK = 256
CHUNKS = PAIRS * N // CHUNK
LEAD = WINDOW - CHUNK
LOADS = (128, 128)
FIRST_PIECES = (64, 64, 64, 64)
SCALAR_PIECE = 128
SINGLE = ((1, 0), (3, 0), (3, 1))
PIECES = (128, 64, 64)


def tile_rows_glin_sigmoid_kernel(tc, x, w_words, w_scales, out):
    nc = tc.nc
    x_v = x.rearrange("(s c) (p j) n -> s (c p) j n", c=SIDE, j=PACK)
    words_v = w_words.rearrange("(s c) p b -> (c p) s b", c=SIDE)
    scales_v = w_scales.rearrange("(s c) (h r) m -> (c h) r s m", c=SIDE, r=SCALE_ROWS)
    out_v = out.rearrange("(s c) (t p) n -> s p c t n", c=SIDE, p=M_TILE)

    with ExitStack() as ctx:
        sb = ctx.enter_context(tc.tile_pool(name="sb", bufs=1))
        ps = ctx.enter_context(tc.psum_pool(name="ps", bufs=1))
        ctx.enter_context(tc.manual_schedule())

        words = []
        for s in range(PAIRS):
            words.append(sb.tile([P, 2 * M], U8, align_bytes=ALIGN, name="words%d" % s))
        w_plane = sb.tile([P, PAIRS, M], U8, align_bytes=ALIGN, name="w_plane")
        codes = sb.tile([P, LEAD + PAIRS * N], U32, align_bytes=ALIGN, name="codes")
        x_plane = sb.tile([P, LEAD + PAIRS * N], U8, align_bytes=ALIGN, name="x_plane")
        raw = []
        grouped = []
        res = []
        for k in range(CHUNKS):
            for i, width in enumerate(LOADS if k > 0 else (CHUNK,)):
                first = k * CHUNK + sum(LOADS[:i])
                tile = sb.tile([P, PACK, width], F32, align_bytes=ALIGN, name="raw%d" % first)
                raw.append((first, width, tile))
            grouped.append(sb.tile([P, CHUNK, PACK], BF16, align_bytes=ALIGN, name="grouped%d" % k))
            res.append(sb.tile([P, SIDE, M_TILES, CHUNK], F32, align_bytes=ALIGN, name="res%d" % k))
        acc = {}
        for b in range(BANKS):
            for c in range(SIDE):
                acc[c, b] = ps.tile([M_TILE, WINDOW], F32, name="acc%d_%d" % (b, c))
        used = [[] for c in range(SIDE)]

        nc.vector.memset(w_plane[:].rearrange("p s m -> p (s m)").bitcast(I32), 0)
        warm = sb.tile([P, 2], F32, align_bytes=ALIGN, name="warm")
        nc.vector.memset(warm[:, 0:1], 0.0)
        nc.scalar.activation(out=warm[:, 1:2], in_=warm[:, 0:1], func=SIGMOID)
        nc.vector.memset(codes[:, 0:LEAD], 0)
        nc.vector.memset(x_plane[:, 0:LEAD].bitcast(I32), 0)

        def load_chunk(k):
            for first, width, tile in raw:
                if first // CHUNK == k:
                    nc.sync.dma_start(out=tile[:], in_=x_v[first // N, :, :, first % N:first % N + width])

        def load_words(s):
            nc.sync.dma_start(out=words[s][:].bitcast(I32), in_=words_v[:, s, :].bitcast(I32))

        def load_scales(q):
            nc.sync.dma_start(
                out=w_plane[QUADRANT * q:QUADRANT * q + SCALE_ROWS, :, :].bitcast(I32),
                in_=scales_v[q].bitcast(I32),
            )

        load_chunk(0)
        load_words(0)
        for q in range(P // QUADRANT):
            load_scales(q)
        load_chunk(1)
        load_chunk(2)
        load_words(1)
        load_chunk(3)

        def interleave(lo, n, copy):
            for first, width, tile in raw:
                if first <= lo < first + width:
                    copy(
                        out=grouped[lo // CHUNK][:, lo % CHUNK:lo % CHUNK + n, :].rearrange("p (c i) t -> p c t i", i=RUN),
                        in_=tile[:, :, lo - first:lo - first + n].rearrange("p t (c i) -> p c t i", i=RUN),
                    )

        def quantise(lo, n):
            cols = slice(LEAD + lo, LEAD + lo + n)
            nc.vector.quantize_mx(
                out=codes[:, cols].bitcast(FP8X4),
                scales=x_plane[:, cols],
                in_=grouped[lo // CHUNK][:, lo % CHUNK:lo % CHUNK + n, :].rearrange("p n t -> p (n t)"),
            )

        def prepare(lo, pieces):
            cuts = [(lo + sum(pieces[:i]), n) for i, n in enumerate(pieces)]
            for start, n in cuts:
                interleave(start, n, nc.scalar.copy if start == SCALAR_PIECE else nc.vector.tensor_copy)
            for start, n in cuts:
                quantise(start, n)

        def multiply(lo, n, mt, c):
            s = lo // N
            window = slice(LEAD + lo + n - WINDOW, LEAD + lo + n)
            rows = slice(c * ROWS, (c + 1) * ROWS)
            bank = acc[c, len(used[c]) % BANKS]
            used[c].append(bank)
            nc.tensor.matmul_mx(
                out=bank[:],
                lhsT=words[s][rows, 2 * M_TILE * mt:2 * M_TILE * (mt + 1)].bitcast(FP4X4),
                lhsT_scale=w_plane[rows, s, M_TILE * mt:M_TILE * (mt + 1)],
                rhs=codes[rows, window].bitcast(FP8X4),
                rhs_scale=x_plane[rows, window],
                start=True,
                stop=True,
            )
            nc.scalar.activation(
                out=res[lo // CHUNK][:, c, mt, lo % CHUNK:lo % CHUNK + n],
                in_=bank[:, WINDOW - n:WINDOW],
                func=SIGMOID,
            )

        def store_tile(k, mt):
            first = k * CHUNK % N
            nc.sync.dma_start(out=out_v[k * CHUNK // N, :, :, mt, first:first + CHUNK], in_=res[k][:, :, mt, :])

        def store_one(k, mt, c):
            first = k * CHUNK % N
            nc.sync.dma_start(out=out_v[k * CHUNK // N, :, c, mt, first:first + CHUNK], in_=res[k][:, c, mt, :])

        for k in range(CHUNKS):
            lo = k * CHUNK
            prepare(lo, PIECES if k > 0 else FIRST_PIECES)
            for mt in range(M_TILES):
                for c in range(SIDE):
                    multiply(lo, CHUNK, mt, c)
                    if (k, mt) in SINGLE:
                        store_one(k, mt, c)
                if (k, mt) not in SINGLE:
                    store_tile(k, mt)
